import numpy as np, ml_dtypes
CORES = [0,1,2,3]
N = 4
def setup_inputs(rng):
    return {"x": rng.standard_normal((N, 128, 128), dtype=np.float32).astype(ml_dtypes.bfloat16)}
def reference(x):
    p = 128 // N
    blocks = x.reshape(N, N, p, 128)
    return {"y": np.ascontiguousarray(blocks.transpose(1, 0, 2, 3)).reshape(N, 128, 128)}

@@ -1,0 +1,42 @@
+from concourse.bass import DstId, RemoteDMATransfer
+
+N = 4
+P = 128 // N
+
+SCRATCH = {
+    "send": ("dram", [N, 128, P], "bfloat16"),
+    "recv": ("dram", [N, 128, P], "bfloat16"),
+}
+SEMAPHORES = ["loaded", "sent", "arrived", "stored"]
+
+ENGINES = {1: 0x000F, 2: 0x00F0, 3: 0xFF00}
+ENGINE_SUM = 16
+
+
+def rank_program(g, core, T, topo):
+    r = T.rank_of(core)
+    if r is None:
+        return
+    runs = [(a, b) for (a, b) in ((0, r), (r + 1, N)) if a < b]
+    queues = [g.sync, g.scalar]
+
+    for q, (a, b) in zip(queues, runs):
+        q.dma_start(T.send[a:b], T.x[P * a:P * b, :]).then_inc(T.sem.loaded, 16)
+    queues[-1].dma_start(T.y[P * r:P * (r + 1), :], T.x[P * r:P * (r + 1), :]).then_inc(T.sem.stored, 16)
+
+    g.wait_ge(T.sem.loaded, 16 * len(runs))
+    transfers = []
+    for d in range(1, N):
+        j = (r + d) % N
+        rid, pid, _se = topo.addr(T.cores[j])
+        transfers.append(RemoteDMATransfer(dst_ids=[DstId(rid=rid, pnc=pid)], dma_engine_mask=ENGINES[d],
+                                           remote_sem=T.sem.arrived, src=T.send[j], dst=T.recv[r]))
+    g.remote_dma_fused(transfers, local_sem=T.sem.sent)
+
+    for q, (a, b) in zip(queues, runs):
+        q.wait_ge(T.sem.arrived, ENGINE_SUM)
+        q.dma_start(T.y[P * a:P * b, :], T.recv[a:b]).then_inc(T.sem.stored, 16)
+
+    g.wait_ge(T.sem.sent, ENGINE_SUM)
+    g.wait_ge(T.sem.arrived, ENGINE_SUM)
+    g.wait_ge(T.sem.stored, 16 * (len(runs) + 1))

@@ -7,7 +7,7 @@ SCRATCH = {
     "send": ("dram", [N, 128, P], "bfloat16"),
     "recv": ("dram", [N, 128, P], "bfloat16"),
 }
-SEMAPHORES = ["loaded", "sent", "arrived", "stored"]
+SEMAPHORES = ["loaded", "own", "sent", "arrived", "stored"]
 
 ENGINES = {1: 0x000F, 2: 0x00F0, 3: 0xFF00}
 ENGINE_SUM = 16
@@ -17,14 +17,13 @@ def rank_program(g, core, T, topo):
     r = T.rank_of(core)
     if r is None:
         return
-    runs = [(a, b) for (a, b) in ((0, r), (r + 1, N)) if a < b]
-    queues = [g.sync, g.scalar]
 
-    for q, (a, b) in zip(queues, runs):
-        q.dma_start(T.send[a:b], T.x[P * a:P * b, :]).then_inc(T.sem.loaded, 16)
-    queues[-1].dma_start(T.y[P * r:P * (r + 1), :], T.x[P * r:P * (r + 1), :]).then_inc(T.sem.stored, 16)
+    a = 1 if r == 0 else 0
+    b = N - 1 if r == N - 1 else N
+    g.sync.dma_start(T.send[a:b], T.x[P * a:P * b, :]).then_inc(T.sem.loaded, 16)
+    g.scalar.dma_start(T.recv[r], T.x[P * r:P * (r + 1), :]).then_inc(T.sem.own, 16)
 
-    g.wait_ge(T.sem.loaded, 16 * len(runs))
+    g.wait_ge(T.sem.loaded, 16)
     transfers = []
     for d in range(1, N):
         j = (r + d) % N
@@ -33,10 +32,9 @@ def rank_program(g, core, T, topo):
                                            remote_sem=T.sem.arrived, src=T.send[j], dst=T.recv[r]))
     g.remote_dma_fused(transfers, local_sem=T.sem.sent)
 
-    for q, (a, b) in zip(queues, runs):
-        q.wait_ge(T.sem.arrived, ENGINE_SUM)
-        q.dma_start(T.y[P * a:P * b, :], T.recv[a:b]).then_inc(T.sem.stored, 16)
+    g.sync.wait_ge(T.sem.own, 16)
+    g.sync.wait_ge(T.sem.arrived, ENGINE_SUM)
+    g.sync.dma_start(T.y[:, :], T.recv[:]).then_inc(T.sem.stored, 16)
 
     g.wait_ge(T.sem.sent, ENGINE_SUM)
-    g.wait_ge(T.sem.arrived, ENGINE_SUM)
-    g.wait_ge(T.sem.stored, 16 * (len(runs) + 1))
+    g.wait_ge(T.sem.stored, 16)

from concourse.bass import DstId, RemoteDMATransfer

N = 4
P = 128 // N

SCRATCH = {
    "send": ("dram", [N, 128, P], "bfloat16"),
    "recv": ("dram", [N, 128, P], "bfloat16"),
}
SEMAPHORES = ["loaded", "own", "sent", "arrived", "stored"]

ENGINES = {1: 0x000F, 2: 0x00F0, 3: 0xFF00}
ENGINE_SUM = 16


def rank_program(g, core, T, topo):
    r = T.rank_of(core)
    if r is None:
        return

    a = 1 if r == 0 else 0
    b = N - 1 if r == N - 1 else N
    g.sync.dma_start(T.send[a:b], T.x[P * a:P * b, :]).then_inc(T.sem.loaded, 16)
    g.scalar.dma_start(T.recv[r], T.x[P * r:P * (r + 1), :]).then_inc(T.sem.own, 16)

    g.wait_ge(T.sem.loaded, 16)
    transfers = []
    for d in range(1, N):
        j = (r + d) % N
        rid, pid, _se = topo.addr(T.cores[j])
        transfers.append(RemoteDMATransfer(dst_ids=[DstId(rid=rid, pnc=pid)], dma_engine_mask=ENGINES[d],
                                           remote_sem=T.sem.arrived, src=T.send[j], dst=T.recv[r]))
    g.remote_dma_fused(transfers, local_sem=T.sem.sent)

    g.sync.wait_ge(T.sem.own, 16)
    g.sync.wait_ge(T.sem.arrived, ENGINE_SUM)
    g.sync.dma_start(T.y[:, :], T.recv[:]).then_inc(T.sem.stored, 16)

    g.wait_ge(T.sem.sent, ENGINE_SUM)
    g.wait_ge(T.sem.stored, 16)
